import numpy as np
import ml_dtypes


def mxq(x, axis, fmt="e4m3"):
    dtype, down = {"e4m3": (ml_dtypes.float8_e4m3fn, 7), "e5m2": (ml_dtypes.float8_e5m2, 14)}[fmt]
    v = np.moveaxis(np.asarray(x, np.float32).astype(ml_dtypes.bfloat16).astype(np.float64), axis, -1)
    blocks = v.reshape(v.shape[:-1] + (-1, 32))
    amax = np.abs(blocks).max(-1, keepdims=True)
    byte = np.maximum(np.where(amax > 0, np.frexp(amax)[1] - 1 + 127, 0) - down, 1)
    scale = np.exp2(byte - 127.0)
    codes = (blocks / scale).astype(np.float32).astype(dtype).astype(np.float64)
    return np.moveaxis((codes * scale).reshape(v.shape), -1, axis)


WIDE = False


def mx_kscale(k):
    if not WIDE:
        return np.ones(k)
    levels = np.array([10, -10, 5, -5, 0])
    if k % 512:
        return np.exp2(np.random.permutation(np.resize(levels, k // 32))).repeat(32)
    a = np.empty((k // 512, 16))
    for p in range(k // 512):
        a[p, :8] = np.random.permutation(np.resize(levels, 8))
        for g in range(8):
            far = levels[np.abs(levels - a[p, g]) >= 10]
            a[p, g + 8] = far[np.random.randint(len(far))]
    return np.exp2(a.ravel()).repeat(32)


def f64(x):
    return np.asarray(x).astype(np.float64)


def striped(idx):
    return np.tile(idx.reshape(-1, 16).T, (8, 1)).astype(np.uint16)


def unstriped(offs):
    return offs[:16].T.reshape(-1).astype(np.int64)


E2M1 = np.array([0.0, 0.5, 1.0, 1.5, 2.0, 3.0, 4.0, 6.0, -0.0, -0.5, -1.0, -1.5, -2.0, -3.0, -4.0, -6.0])


def pack_weight(w, fmt):
    k, n = w.shape
    w = f64(np.asarray(w, np.float32).astype(ml_dtypes.bfloat16)).reshape(k // 32, 32, n)
    amax = np.abs(w).max(1)
    if fmt == "e4m3":
        byte = np.frexp(amax)[1] - 1 + 127 - 7
    else:
        mant, ex = np.frexp(amax / 6.0)
        byte = np.where(mant > 0.5, ex, ex - 1) + 127
    byte = np.clip(np.where(amax > 0, byte, 1), 1, 254)
    scaled = (w * np.exp2(127.0 - byte)[:, None, :]).reshape(k, n).astype(np.float32)
    by_word = np.ascontiguousarray(scaled.reshape(k // 512, 128, 4, n).transpose(0, 1, 3, 2))
    if fmt == "e4m3":
        words = by_word.astype(ml_dtypes.float8_e4m3fn).view(np.uint8)
    else:
        c = by_word.astype(ml_dtypes.float4_e2m1fn).view(np.uint8) & 0xF
        words = (c[..., 0::2] | (c[..., 1::2] << 4)).reshape(k // 512, 128, 2 * n)
    return np.ascontiguousarray(words), np.ascontiguousarray(byte.astype(np.uint8).reshape(k // 512, 16, n))


def unpack_weight(words, scales, fmt):
    g, _, n = scales.shape
    words = np.ascontiguousarray(words).reshape(g, 128, n, -1)
    if fmt == "e4m3":
        vals = words.view(ml_dtypes.float8_e4m3fn).astype(np.float64)
    else:
        nib = np.empty((g, 128, n, 4), np.uint8)
        nib[..., 0::2] = words & 0xF
        nib[..., 1::2] = words >> 4
        vals = E2M1[nib]
    vals = vals * np.repeat(np.exp2(scales.astype(np.float64) - 127.0), 8, axis=1)[..., None]
    return vals.transpose(0, 1, 3, 2).reshape(g * 512, n)


def gelu(v):
    return 0.5 * v * (1.0 + np.tanh(np.sqrt(2.0 / np.pi) * (v + 0.044715 * v**3)))


K, T, S, P, P2, H, N = 1024, 4096, 2048, 1024, 512, 512, 768

def setup_inputs():
    n = np.random.standard_normal
    s = mx_kscale(K)[:, None]
    u = mx_kscale(H)[:, None]
    tab_words, tab_scales = pack_weight(n((K, T)) * s, "e4m3")
    w4_words, w4_scales = pack_weight(1.2 * n((K, H)) / np.sqrt(K) / s * u.T, "e2m1")
    return {
        "tab_words": tab_words,
        "tab_scales": tab_scales,
        "offs": striped(np.random.permutation(T)[:S]),
        "pos1": striped(np.random.permutation(S)[:P]),
        "pos2": striped(np.random.permutation(S)[:P]),
        "pos3": striped(np.random.permutation(P)[:P2]),
        "pos4": striped(np.random.permutation(S)[:P2]),
        "w1": (1.2 * n((K, H)) / np.sqrt(K) / s * u.T).astype(np.float32),
        "w4_words": w4_words,
        "w4_scales": w4_scales,
        "trust": (1.3 * np.exp(0.3 * n(H)) / u[:, 0]).astype(np.float32),
        "w2": (n((H, N)) / np.sqrt(H) / u).astype(np.float32),
        "desk": (0.8 * n((N, P2))).astype(np.float32),
    }

def reference(tab_words, tab_scales, offs, pos1, pos2, pos3, pos4, w1, w4_words, w4_scales, trust, w2, desk):
    v = unpack_weight(tab_words, tab_scales, "e4m3")[:, unstriped(offs)]
    w4 = unpack_weight(w4_words, w4_scales, "e2m1")
    q1 = mxq(f64(w1), 0, "e4m3")
    h = np.maximum(q1.T @ v, w4.T @ v)
    source = np.tanh(f64(trust)[:, None] * h[:, unstriped(pos2)])
    a1 = h[:, unstriped(pos1)] * source
    a2 = a1[:, unstriped(pos3)] - h[:, unstriped(pos4)]
    q2 = mxq(f64(w2), 0, "e4m3")
    urgency = q2.T @ mxq(a2, 0, "e4m3")
    return urgency + f64(desk)

@@ -1,0 +1,243 @@
+from contextlib import ExitStack
+
+import concourse.mybir as mybir
+
+K, T, S, PAIRS, KEPT, H, N = 1024, 4096, 2048, 1024, 512, 512, 768
+FLOPS = 2 * (2 * K * H * S + H * N * KEPT)
+
+F32 = mybir.dt.float32
+BF16 = mybir.dt.bfloat16
+I32 = mybir.dt.int32
+U32 = mybir.dt.uint32
+U16 = mybir.dt.uint16
+U8 = mybir.dt.uint8
+FP8X4 = mybir.dt.float8_e4m3fn_x4
+FP4X4 = mybir.dt.float4_e2m1fn_x4
+ALU = mybir.AluOpType
+ACT = mybir.ActivationFunctionType
+
+P = 128
+PACK = 4
+PASSES = K // (P * PACK)
+BANK = 512
+CHUNKS = S // BANK
+HALF = KEPT // 2
+N_TILES = N // P
+LIST_ROWS = 16
+SCALE_ROWS = 16
+
+
+def tile_list_claim_triage_urgency_kernel(
+    tc, tab_words, tab_scales, offs, pos1, pos2, pos3, pos4, w1, w4_words, w4_scales, trust, w2, desk, out
+):
+    nc = tc.nc
+    with ExitStack() as ctx:
+        lists = ctx.enter_context(tc.tile_pool(name="lists", bufs=1))
+        keep = ctx.enter_context(tc.tile_pool(name="keep", bufs=1))
+        work = ctx.enter_context(tc.tile_pool(name="work", bufs=2))
+        psum = ctx.enter_context(tc.psum_pool(name="psum", bufs=4))
+
+        def load_list(src, name):
+            tile = lists.tile([P, src.shape[1]], U16, name=name)
+            nc.sync.dma_start(tile[:], src)
+            return tile
+
+        idx = load_list(offs, "idx")
+        tab_sc = keep.tile([P, T // 4], I32, name="tab_sc", align_bytes=64)
+        nc.sync.dma_start(
+            out=tab_sc[0 : PASSES * SCALE_ROWS, :], in_=tab_scales.rearrange("a q t -> q a t").bitcast(I32)
+        )
+        nc.vector.memset(tab_sc[32:64, :], 0)
+        nc.gpsimd.memset(tab_sc[64:128, :], 0)
+        tab = []
+        for a in range(PASSES):
+            words = keep.tile([P, T], I32, name="tab%d" % a, tag="tab%d" % a, align_bytes=64)
+            nc.sync.dma_start(out=words[:], in_=tab_words[a].rearrange("p t i -> p (t i)").bitcast(I32))
+            tab.append(words)
+        w4w_raw = keep.tile([P, PASSES, 2 * H // 4], I32, name="w4w_raw")
+        nc.sync.dma_start(out=w4w_raw[:], in_=w4_words.rearrange("a p c -> p a c").bitcast(I32))
+        w4s_raw = keep.tile([P, PASSES, H // 4], I32, name="w4s_raw")
+        for q in range(4):
+            nc.sync.dma_start(
+                out=w4s_raw[32 * q : 32 * q + 4, :, :],
+                in_=w4_scales[:, 4 * q : 4 * q + 4, :].rearrange("a r c -> r a c").bitcast(I32),
+            )
+        w1_raw = []
+        for a in range(PASSES):
+            rows = keep.tile([P, PACK, H], F32, name="w1_raw%d" % a)
+            nc.sync.dma_start(out=rows[:], in_=w1[a * 512 : (a + 1) * 512, :].rearrange("(p j) c -> p j c", j=PACK))
+            w1_raw.append(rows)
+
+        picked_sc = keep.tile([P, S // 4], I32, name="picked_sc", align_bytes=64)
+        nc.vector.tensor_copy(picked_sc[:].bitcast(U8), tab_sc[:].bitcast(U8).indirect(idx[:]))
+        planes = keep.tile([P, PASSES * S // 4], I32, name="planes", align_bytes=64)
+        nc.gpsimd.memset(planes[:], 0)
+        for q in range(4):
+            nc.gpsimd.dma_start(out=planes[32 * q : 32 * q + 4, :], in_=picked_sc[8 * q : 8 * q + 8, :])
+        v_scales = planes[:].bitcast(U8)
+
+        picked = [keep.tile([P, S], U32, name="picked%d" % a, align_bytes=64) for a in range(PASSES)]
+        nc.vector.tensor_copy(picked[0][:], tab[0][:].bitcast(U32).indirect(idx[:]))
+        cols = BANK // LIST_ROWS
+        for c in range(CHUNKS):
+            nc.vector.tensor_copy(
+                picked[1][:, c * BANK : (c + 1) * BANK],
+                tab[1][:].bitcast(U32).indirect(idx[:, c * cols : (c + 1) * cols]),
+            )
+
+        p2 = load_list(pos2, "p2")
+        p4 = load_list(pos4, "p4")
+        p1 = load_list(pos1, "p1")
+        p3 = load_list(pos3, "p3")
+        trust_sb = []
+        for t in range(PACK):
+            column = keep.tile([P, 1], F32, name="trust%d" % t)
+            with nc.allow_non_contiguous_dma(reason="one float a partition"):
+                nc.sync.dma_start(out=column[:], in_=trust.rearrange("(g t u) -> t g u", t=PACK, u=8)[t])
+            trust_sb.append(column)
+
+        w4w = keep.tile([P, PASSES, 2 * H // 4], I32, name="w4w", align_bytes=64)
+        nc.gpsimd.tensor_copy(
+            out=w4w[:].rearrange("p a (t g w) -> p a t g w", t=PACK, w=4),
+            in_=w4w_raw[:].rearrange("p a (g t w) -> p a t g w", t=PACK, w=4),
+        )
+        w4s = keep.tile([P, PASSES, H // 4], I32, name="w4s", align_bytes=64)
+        nc.gpsimd.memset(w4s[:], 0)
+        for q in range(4):
+            rows = slice(32 * q, 32 * q + 4)
+            nc.gpsimd.tensor_copy(
+                out=w4s[rows, :, :].rearrange("p a (t g w) -> p a t g w", t=PACK, w=2),
+                in_=w4s_raw[rows, :, :].rearrange("p a (g t w) -> p a t g w", t=PACK, w=2),
+            )
+
+        w1_codes, w1_scales = [], []
+        for t in range(PACK):
+            grouped = work.tile([P, PASSES, P * PACK], BF16, name="w1_grouped", align_bytes=64)
+            for a in range(PASSES):
+                nc.scalar.copy(
+                    out=grouped[:, a, :].rearrange("p (g u j) -> p g u j", u=8, j=PACK),
+                    in_=w1_raw[a][:].rearrange("p j (g t u) -> p t g u j", t=PACK, u=8)[:, t],
+                )
+            codes = keep.tile([P, PASSES * P], U32, name="w1_codes%d" % t, align_bytes=64)
+            scales = keep.tile([P, PASSES * P], U8, name="w1_scales%d" % t, align_bytes=64)
+            nc.vector.quantize_mx(
+                out=codes[:].bitcast(FP8X4), scales=scales[:], in_=grouped[:].rearrange("p a c -> p (a c)")
+            )
+            w1_codes.append(codes)
+            w1_scales.append(scales)
+
+        def product(acc, weights, weight_scales, c):
+            for a in range(PASSES):
+                nc.tensor.matmul_mx(
+                    out=acc[:],
+                    lhsT=weights(a),
+                    lhsT_scale=weight_scales(a),
+                    rhs=picked[a][:, c * BANK : (c + 1) * BANK].bitcast(FP8X4),
+                    rhs_scale=v_scales[:, a * S + c * BANK : a * S + (c + 1) * BANK],
+                    start=(a == 0),
+                    stop=(a == PASSES - 1),
+                )
+
+        a2_first = keep.tile([P, PACK, HALF], F32, name="a2_first")
+        half_cols = HALF // LIST_ROWS
+        a1_tiles, earlier_tiles = [], []
+        for t in range(PACK):
+            h = keep.tile([P, S], F32, name="h%d" % t)
+            for c in range(CHUNKS):
+                span = slice(c * BANK, (c + 1) * BANK)
+                acc4 = psum.tile([P, BANK], F32, name="acc4", tag="left")
+                product(
+                    acc4,
+                    lambda a: w4w[:, a, 64 * t : 64 * (t + 1)].bitcast(FP4X4),
+                    lambda a: w4s[:, a, 32 * t : 32 * (t + 1)].bitcast(U8),
+                    c,
+                )
+                nc.scalar.copy(out=h[:, span], in_=acc4[:])
+                acc1 = psum.tile([P, BANK], F32, name="acc1", tag="right")
+                product(
+                    acc1,
+                    lambda a: w1_codes[t][:, a * P : (a + 1) * P].bitcast(FP8X4),
+                    lambda a: w1_scales[t][:, a * P : (a + 1) * P],
+                    c,
+                )
+                nc.vector.tensor_tensor(h[:, span], acc1[:], h[:, span], ALU.max)
+
+            partner = work.tile([P, PAIRS], F32, name="partner")
+            nc.vector.tensor_copy(partner[:], h[:].indirect(p2[:]))
+            source = keep.tile([P, PAIRS], F32, name="source", tag="source")
+            nc.scalar.activation(out=source[:], in_=partner[:], func=ACT.Tanh, scale=trust_sb[t][:])
+            earlier = keep.tile([P, KEPT], F32, name="earlier%d" % t)
+            nc.vector.tensor_copy(earlier[:], h[:].indirect(p4[:]))
+            a1 = keep.tile([P, PAIRS], F32, name="a1_%d" % t)
+            nc.vector.tensor_tensor(a1[:], h[:].indirect(p1[:]), source[:], ALU.mult)
+            nc.vector.tensor_tensor(
+                a2_first[:, t, :], a1[:].indirect(p3[:, 0:half_cols]), earlier[:, 0:HALF], ALU.subtract
+            )
+            a1_tiles.append(a1)
+            earlier_tiles.append(earlier)
+
+        w2_raw = keep.tile([P, PACK, N], F32, name="w2_raw", tag="tab0", align_bytes=64)
+        for t in range(PACK):
+            nc.sync.dma_start(out=w2_raw[:, t, :], in_=w2.rearrange("(g t u) n -> t g u n", t=PACK, u=8)[t])
+        desk_sb = keep.tile([P, N_TILES, KEPT], F32, name="desk_sb", tag="tab1", align_bytes=64)
+        nc.sync.dma_start(out=desk_sb[:], in_=desk.rearrange("(i p) j -> p i j", p=P))
+        w2_grouped = keep.tile([P, N, PACK], BF16, name="w2_grouped", align_bytes=64)
+        for i in range(N_TILES):
+            span = slice(i * P, (i + 1) * P)
+            nc.scalar.copy(out=w2_grouped[:, span, :], in_=w2_raw[:, :, span].rearrange("p t n -> p n t"))
+        w2_codes = keep.tile([P, N], U32, name="w2_codes", align_bytes=64)
+        w2_scales = keep.tile([P, N], U8, name="w2_scales", align_bytes=64)
+        for i in range(2):
+            span = slice(i * N // 2, (i + 1) * N // 2)
+            nc.vector.quantize_mx(
+                out=w2_codes[:, span].bitcast(FP8X4),
+                scales=w2_scales[:, span],
+                in_=w2_grouped[:, span, :].rearrange("p n t -> p (n t)"),
+            )
+
+        out_rows = out.rearrange("(i p) j -> p i j", p=P)
+
+        def second_stage(a2, half, bank_tag):
+            grouped = work.tile([P, HALF, PACK], BF16, name="a2_grouped", align_bytes=64)
+            nc.scalar.copy(out=grouped[:], in_=a2[:].rearrange("p t j -> p j t"))
+            codes = work.tile([P, HALF], U32, name="a2_codes", align_bytes=64)
+            scales = work.tile([P, HALF], U8, name="a2_scales", align_bytes=64)
+            nc.vector.quantize_mx(
+                out=codes[:].bitcast(FP8X4), scales=scales[:], in_=grouped[:].rearrange("p j t -> p (j t)")
+            )
+            banks = []
+            for b in range(N_TILES // 2):
+                acc = psum.tile([P, 2, HALF], F32, name="acc2", tag=bank_tag)
+                for e in range(2):
+                    span = slice((2 * b + e) * P, (2 * b + e + 1) * P)
+                    nc.tensor.matmul_mx(
+                        out=acc[:, e, :],
+                        lhsT=w2_codes[:, span].bitcast(FP8X4),
+                        lhsT_scale=w2_scales[:, span],
+                        rhs=codes[:].bitcast(FP8X4),
+                        rhs_scale=scales[:],
+                        start=True,
+                        stop=True,
+                    )
+                banks.append(acc)
+            return banks
+
+        def finish(banks, half):
+            span = slice(half * HALF, (half + 1) * HALF)
+            for b, acc in enumerate(banks):
+                result = work.tile([P, 2, HALF], F32, name="result", bufs=6)
+                nc.vector.tensor_tensor(result[:], acc[:], desk_sb[:, 2 * b : 2 * b + 2, span], ALU.add)
+                nc.sync.dma_start(out=out_rows[:, 2 * b : 2 * b + 2, span], in_=result[:])
+
+        first_banks = second_stage(a2_first, 0, "left")
+        a2_second = keep.tile([P, PACK, HALF], F32, name="a2_second", tag="source")
+        for t in range(PACK):
+            nc.vector.tensor_tensor(
+                a2_second[:, t, :],
+                a1_tiles[t][:].indirect(p3[:, half_cols : 2 * half_cols]),
+                earlier_tiles[t][:, HALF:KEPT],
+                ALU.subtract,
+            )
+        second_banks = second_stage(a2_second, 1, "right")
+        finish(first_banks, 0)
+        finish(second_banks, 1)

@@ -42,39 +42,51 @@ def tile_list_claim_triage_urgency_kernel(
             nc.sync.dma_start(tile[:], src)
             return tile
 
-        idx = load_list(offs, "idx")
-        tab_sc = keep.tile([P, T // 4], I32, name="tab_sc", align_bytes=64)
-        nc.sync.dma_start(
-            out=tab_sc[0 : PASSES * SCALE_ROWS, :], in_=tab_scales.rearrange("a q t -> q a t").bitcast(I32)
-        )
-        nc.vector.memset(tab_sc[32:64, :], 0)
-        nc.gpsimd.memset(tab_sc[64:128, :], 0)
-        tab = []
-        for a in range(PASSES):
-            words = keep.tile([P, T], I32, name="tab%d" % a, tag="tab%d" % a, align_bytes=64)
-            nc.sync.dma_start(out=words[:], in_=tab_words[a].rearrange("p t i -> p (t i)").bitcast(I32))
-            tab.append(words)
-        w4w_raw = keep.tile([P, PASSES, 2 * H // 4], I32, name="w4w_raw")
-        nc.sync.dma_start(out=w4w_raw[:], in_=w4_words.rearrange("a p c -> p a c").bitcast(I32))
-        w4s_raw = keep.tile([P, PASSES, H // 4], I32, name="w4s_raw")
+        w4s_raw = keep.tile([P, PASSES, H // 4], U32, name="w4s_raw")
         for q in range(4):
-            nc.sync.dma_start(
-                out=w4s_raw[32 * q : 32 * q + 4, :, :],
+            nc.gpsimd.dma_start(
+                out=w4s_raw[32 * q : 32 * q + 4, :, :].bitcast(I32),
                 in_=w4_scales[:, 4 * q : 4 * q + 4, :].rearrange("a r c -> r a c").bitcast(I32),
             )
-        w1_raw = []
-        for a in range(PASSES):
-            rows = keep.tile([P, PACK, H], F32, name="w1_raw%d" % a)
-            nc.sync.dma_start(out=rows[:], in_=w1[a * 512 : (a + 1) * 512, :].rearrange("(p j) c -> p j c", j=PACK))
-            w1_raw.append(rows)
+        idx = load_list(offs, "idx")
+        tab_sc = keep.tile([P, T // 4], I32, name="tab_sc", tag="tab_sc", align_bytes=64)
+        nc.sync.dma_start(
+            out=tab_sc[P - PASSES * SCALE_ROWS : P, :], in_=tab_scales.rearrange("a q t -> q a t").bitcast(I32)
+        )
+        nc.vector.memset(tab_sc[0 : P - PASSES * SCALE_ROWS, :], 0)
+        p2 = load_list(pos2, "p2")
+        p4 = load_list(pos4, "p4")
+        p1 = load_list(pos1, "p1")
+        p3 = load_list(pos3, "p3")
+
+        def load_words(a):
+            words = keep.tile([P, T], I32, name="tab%d" % a, tag="tab%d" % a, align_bytes=64)
+            nc.sync.dma_start(out=words[:], in_=tab_words[a].rearrange("p t i -> p (t i)").bitcast(I32))
+            return words
+
+        tab = [load_words(0)]
+        trust_sb = []
+        for t in range(PACK):
+            column = keep.tile([P, 1], F32, name="trust%d" % t)
+            with nc.allow_non_contiguous_dma(reason="one float a partition"):
+                nc.gpsimd.dma_start(out=column[:], in_=trust.rearrange("(g t u) -> t g u", t=PACK, u=8)[t])
+            trust_sb.append(column)
+        w4w_raw = keep.tile([P, PASSES, 2 * H // 4], U32, name="w4w_raw")
+        nc.sync.dma_start(out=w4w_raw[:].bitcast(I32), in_=w4_words.rearrange("a p c -> p a c").bitcast(I32))
+        tab.append(load_words(1))
 
         picked_sc = keep.tile([P, S // 4], I32, name="picked_sc", align_bytes=64)
         nc.vector.tensor_copy(picked_sc[:].bitcast(U8), tab_sc[:].bitcast(U8).indirect(idx[:]))
         planes = keep.tile([P, PASSES * S // 4], I32, name="planes", align_bytes=64)
-        nc.gpsimd.memset(planes[:], 0)
+        nc.vector.memset(planes[:], 0)
         for q in range(4):
-            nc.gpsimd.dma_start(out=planes[32 * q : 32 * q + 4, :], in_=picked_sc[8 * q : 8 * q + 8, :])
+            nc.sync.dma_start(out=planes[32 * q : 32 * q + 4, :], in_=picked_sc[96 + 8 * q : 96 + 8 * q + 8, :])
         v_scales = planes[:].bitcast(U8)
+        w1_raw = keep.tile([P, PASSES, PACK, H], F32, name="w1_raw", tag="tab_sc", align_bytes=64)
+        for a in range(PASSES):
+            nc.sync.dma_start(
+                out=w1_raw[:, a], in_=w1[a * 512 : (a + 1) * 512, :].rearrange("(p j) c -> p j c", j=PACK)
+            )
 
         picked = [keep.tile([P, S], U32, name="picked%d" % a, align_bytes=64) for a in range(PASSES)]
         nc.vector.tensor_copy(picked[0][:], tab[0][:].bitcast(U32).indirect(idx[:]))
@@ -85,46 +97,37 @@ def tile_list_claim_triage_urgency_kernel(
                 tab[1][:].bitcast(U32).indirect(idx[:, c * cols : (c + 1) * cols]),
             )
 
-        p2 = load_list(pos2, "p2")
-        p4 = load_list(pos4, "p4")
-        p1 = load_list(pos1, "p1")
-        p3 = load_list(pos3, "p3")
-        trust_sb = []
-        for t in range(PACK):
-            column = keep.tile([P, 1], F32, name="trust%d" % t)
-            with nc.allow_non_contiguous_dma(reason="one float a partition"):
-                nc.sync.dma_start(out=column[:], in_=trust.rearrange("(g t u) -> t g u", t=PACK, u=8)[t])
-            trust_sb.append(column)
-
-        w4w = keep.tile([P, PASSES, 2 * H // 4], I32, name="w4w", align_bytes=64)
-        nc.gpsimd.tensor_copy(
+        w4w = keep.tile([P, PASSES, 2 * H // 4], U32, name="w4w", align_bytes=64)
+        nc.scalar.copy(
             out=w4w[:].rearrange("p a (t g w) -> p a t g w", t=PACK, w=4),
             in_=w4w_raw[:].rearrange("p a (g t w) -> p a t g w", t=PACK, w=4),
         )
-        w4s = keep.tile([P, PASSES, H // 4], I32, name="w4s", align_bytes=64)
-        nc.gpsimd.memset(w4s[:], 0)
+        w4s = keep.tile([P, PASSES, H // 4], U32, name="w4s", align_bytes=64)
+        nc.vector.memset(w4s[:], 0)
         for q in range(4):
             rows = slice(32 * q, 32 * q + 4)
-            nc.gpsimd.tensor_copy(
+            nc.scalar.copy(
                 out=w4s[rows, :, :].rearrange("p a (t g w) -> p a t g w", t=PACK, w=2),
                 in_=w4s_raw[rows, :, :].rearrange("p a (g t w) -> p a t g w", t=PACK, w=2),
             )
 
-        w1_codes, w1_scales = [], []
-        for t in range(PACK):
-            grouped = work.tile([P, PASSES, P * PACK], BF16, name="w1_grouped", align_bytes=64)
+        w1_codes = keep.tile([P, PACK * PASSES * P], U32, name="w1_codes", align_bytes=64)
+        w1_scales = keep.tile([P, PACK * PASSES * P], U8, name="w1_scales", align_bytes=64)
+
+        def quantise_w1(t):
+            grouped = keep.tile([P, PASSES, P * PACK], BF16, name="w1_grouped", tag="tab1", align_bytes=64)
+            interleave = nc.vector.tensor_copy if t == 0 else nc.scalar.copy
             for a in range(PASSES):
-                nc.scalar.copy(
+                interleave(
                     out=grouped[:, a, :].rearrange("p (g u j) -> p g u j", u=8, j=PACK),
-                    in_=w1_raw[a][:].rearrange("p j (g t u) -> p t g u j", t=PACK, u=8)[:, t],
+                    in_=w1_raw[:, a].rearrange("p j (g t u) -> p t g u j", t=PACK, u=8)[:, t],
                 )
-            codes = keep.tile([P, PASSES * P], U32, name="w1_codes%d" % t, align_bytes=64)
-            scales = keep.tile([P, PASSES * P], U8, name="w1_scales%d" % t, align_bytes=64)
+            span = slice(t * PASSES * P, (t + 1) * PASSES * P)
             nc.vector.quantize_mx(
-                out=codes[:].bitcast(FP8X4), scales=scales[:], in_=grouped[:].rearrange("p a c -> p (a c)")
+                out=w1_codes[:, span].bitcast(FP8X4),
+                scales=w1_scales[:, span],
+                in_=grouped[:].rearrange("p a c -> p (a c)"),
             )
-            w1_codes.append(codes)
-            w1_scales.append(scales)
 
         def product(acc, weights, weight_scales, c):
             for a in range(PASSES):
@@ -141,26 +144,30 @@ def tile_list_claim_triage_urgency_kernel(
         a2_first = keep.tile([P, PACK, HALF], F32, name="a2_first")
         half_cols = HALF // LIST_ROWS
         a1_tiles, earlier_tiles = [], []
+        quantise_w1(0)
         for t in range(PACK):
             h = keep.tile([P, S], F32, name="h%d" % t)
             for c in range(CHUNKS):
-                span = slice(c * BANK, (c + 1) * BANK)
-                acc4 = psum.tile([P, BANK], F32, name="acc4", tag="left")
+                acc4 = psum.tile([P, BANK], F32, name="acc4", tag="first")
                 product(
                     acc4,
                     lambda a: w4w[:, a, 64 * t : 64 * (t + 1)].bitcast(FP4X4),
                     lambda a: w4s[:, a, 32 * t : 32 * (t + 1)].bitcast(U8),
                     c,
                 )
-                nc.scalar.copy(out=h[:, span], in_=acc4[:])
-                acc1 = psum.tile([P, BANK], F32, name="acc1", tag="right")
+                nc.scalar.copy(out=h[:, c * BANK : (c + 1) * BANK], in_=acc4[:])
+            for c in range(CHUNKS):
+                span = slice(c * BANK, (c + 1) * BANK)
+                acc1 = psum.tile([P, BANK], F32, name="acc1", tag="first")
                 product(
                     acc1,
-                    lambda a: w1_codes[t][:, a * P : (a + 1) * P].bitcast(FP8X4),
-                    lambda a: w1_scales[t][:, a * P : (a + 1) * P],
+                    lambda a: w1_codes[:, (t * PASSES + a) * P : (t * PASSES + a + 1) * P].bitcast(FP8X4),
+                    lambda a: w1_scales[:, (t * PASSES + a) * P : (t * PASSES + a + 1) * P],
                     c,
                 )
                 nc.vector.tensor_tensor(h[:, span], acc1[:], h[:, span], ALU.max)
+            if t + 1 < PACK:
+                quantise_w1(t + 1)
 
             partner = work.tile([P, PAIRS], F32, name="partner")
             nc.vector.tensor_copy(partner[:], h[:].indirect(p2[:]))
@@ -176,7 +183,7 @@ def tile_list_claim_triage_urgency_kernel(
             a1_tiles.append(a1)
             earlier_tiles.append(earlier)
 
-        w2_raw = keep.tile([P, PACK, N], F32, name="w2_raw", tag="tab0", align_bytes=64)
+        w2_raw = keep.tile([P, PACK, N], F32, name="w2_raw", tag="tab_sc", align_bytes=64)
         for t in range(PACK):
             nc.sync.dma_start(out=w2_raw[:, t, :], in_=w2.rearrange("(g t u) n -> t g u n", t=PACK, u=8)[t])
         desk_sb = keep.tile([P, N_TILES, KEPT], F32, name="desk_sb", tag="tab1", align_bytes=64)
@@ -229,7 +236,7 @@ def tile_list_claim_triage_urgency_kernel(
                 nc.vector.tensor_tensor(result[:], acc[:], desk_sb[:, 2 * b : 2 * b + 2, span], ALU.add)
                 nc.sync.dma_start(out=out_rows[:, 2 * b : 2 * b + 2, span], in_=result[:])
 
-        first_banks = second_stage(a2_first, 0, "left")
+        first_banks = second_stage(a2_first, 0, "second")
         a2_second = keep.tile([P, PACK, HALF], F32, name="a2_second", tag="source")
         for t in range(PACK):
             nc.vector.tensor_tensor(
@@ -238,6 +245,6 @@ def tile_list_claim_triage_urgency_kernel(
                 earlier_tiles[t][:, HALF:KEPT],
                 ALU.subtract,
             )
-        second_banks = second_stage(a2_second, 1, "right")
+        second_banks = second_stage(a2_second, 1, "first")
         finish(first_banks, 0)
         finish(second_banks, 1)

@@ -42,12 +42,6 @@ def tile_list_claim_triage_urgency_kernel(
             nc.sync.dma_start(tile[:], src)
             return tile
 
-        w4s_raw = keep.tile([P, PASSES, H // 4], U32, name="w4s_raw")
-        for q in range(4):
-            nc.gpsimd.dma_start(
-                out=w4s_raw[32 * q : 32 * q + 4, :, :].bitcast(I32),
-                in_=w4_scales[:, 4 * q : 4 * q + 4, :].rearrange("a r c -> r a c").bitcast(I32),
-            )
         idx = load_list(offs, "idx")
         tab_sc = keep.tile([P, T // 4], I32, name="tab_sc", tag="tab_sc", align_bytes=64)
         nc.sync.dma_start(
@@ -65,17 +59,17 @@ def tile_list_claim_triage_urgency_kernel(
             return words
 
         tab = [load_words(0)]
-        trust_sb = []
-        for t in range(PACK):
-            column = keep.tile([P, 1], F32, name="trust%d" % t)
-            with nc.allow_non_contiguous_dma(reason="one float a partition"):
-                nc.gpsimd.dma_start(out=column[:], in_=trust.rearrange("(g t u) -> t g u", t=PACK, u=8)[t])
-            trust_sb.append(column)
         w4w_raw = keep.tile([P, PASSES, 2 * H // 4], U32, name="w4w_raw")
         nc.sync.dma_start(out=w4w_raw[:].bitcast(I32), in_=w4_words.rearrange("a p c -> p a c").bitcast(I32))
+        w4s_raw = keep.tile([P, PASSES, H // 4], U32, name="w4s_raw")
+        for q in range(4):
+            nc.sync.dma_start(
+                out=w4s_raw[32 * q : 32 * q + 4, :, :].bitcast(I32),
+                in_=w4_scales[:, 4 * q : 4 * q + 4, :].rearrange("a r c -> r a c").bitcast(I32),
+            )
         tab.append(load_words(1))
 
-        picked_sc = keep.tile([P, S // 4], I32, name="picked_sc", align_bytes=64)
+        picked_sc = keep.tile([P, S // 4], I32, name="picked_sc", tag="picked_sc", align_bytes=64)
         nc.vector.tensor_copy(picked_sc[:].bitcast(U8), tab_sc[:].bitcast(U8).indirect(idx[:]))
         planes = keep.tile([P, PASSES * S // 4], I32, name="planes", align_bytes=64)
         nc.vector.memset(planes[:], 0)
@@ -87,6 +81,11 @@ def tile_list_claim_triage_urgency_kernel(
             nc.sync.dma_start(
                 out=w1_raw[:, a], in_=w1[a * 512 : (a + 1) * 512, :].rearrange("(p j) c -> p j c", j=PACK)
             )
+
+        trust_sb = keep.tile([P, PACK, 8], F32, name="trust_sb", tag="picked_sc", align_bytes=64)
+        for t in range(PACK):
+            with nc.allow_non_contiguous_dma(reason="one float a partition"):
+                nc.sync.dma_start(out=trust_sb[:, t, 0:1], in_=trust.rearrange("(g t u) -> t g u", t=PACK, u=8)[t])
 
         picked = [keep.tile([P, S], U32, name="picked%d" % a, align_bytes=64) for a in range(PASSES)]
         nc.vector.tensor_copy(picked[0][:], tab[0][:].bitcast(U32).indirect(idx[:]))
@@ -144,6 +143,15 @@ def tile_list_claim_triage_urgency_kernel(
         a2_first = keep.tile([P, PACK, HALF], F32, name="a2_first")
         half_cols = HALF // LIST_ROWS
         a1_tiles, earlier_tiles = [], []
+
+        def kept_pairs(a2, t, half):
+            nc.vector.tensor_tensor(
+                a2[:, t, :],
+                a1_tiles[t][:].indirect(p3[:, half * half_cols : (half + 1) * half_cols]),
+                earlier_tiles[t][:, half * HALF : (half + 1) * HALF],
+                ALU.subtract,
+            )
+
         quantise_w1(0)
         for t in range(PACK):
             h = keep.tile([P, S], F32, name="h%d" % t)
@@ -169,19 +177,21 @@ def tile_list_claim_triage_urgency_kernel(
             if t + 1 < PACK:
                 quantise_w1(t + 1)
 
+            if t > 0:
+                kept_pairs(a2_first, t - 1, 0)
+
             partner = work.tile([P, PAIRS], F32, name="partner")
             nc.vector.tensor_copy(partner[:], h[:].indirect(p2[:]))
             source = keep.tile([P, PAIRS], F32, name="source", tag="source")
-            nc.scalar.activation(out=source[:], in_=partner[:], func=ACT.Tanh, scale=trust_sb[t][:])
+            nc.scalar.activation(out=source[:], in_=partner[:], func=ACT.Tanh, scale=trust_sb[:, t, 0:1])
             earlier = keep.tile([P, KEPT], F32, name="earlier%d" % t)
             nc.vector.tensor_copy(earlier[:], h[:].indirect(p4[:]))
             a1 = keep.tile([P, PAIRS], F32, name="a1_%d" % t)
             nc.vector.tensor_tensor(a1[:], h[:].indirect(p1[:]), source[:], ALU.mult)
-            nc.vector.tensor_tensor(
-                a2_first[:, t, :], a1[:].indirect(p3[:, 0:half_cols]), earlier[:, 0:HALF], ALU.subtract
-            )
             a1_tiles.append(a1)
             earlier_tiles.append(earlier)
+
+        kept_pairs(a2_first, PACK - 1, 0)
 
         w2_raw = keep.tile([P, PACK, N], F32, name="w2_raw", tag="tab_sc", align_bytes=64)
         for t in range(PACK):
@@ -239,12 +249,7 @@ def tile_list_claim_triage_urgency_kernel(
         first_banks = second_stage(a2_first, 0, "second")
         a2_second = keep.tile([P, PACK, HALF], F32, name="a2_second", tag="source")
         for t in range(PACK):
-            nc.vector.tensor_tensor(
-                a2_second[:, t, :],
-                a1_tiles[t][:].indirect(p3[:, half_cols : 2 * half_cols]),
-                earlier_tiles[t][:, HALF:KEPT],
-                ALU.subtract,
-            )
+            kept_pairs(a2_second, t, 1)
         second_banks = second_stage(a2_second, 1, "first")
         finish(first_banks, 0)
         finish(second_banks, 1)

@@ -59,8 +59,6 @@ def tile_list_claim_triage_urgency_kernel(
             return words
 
         tab = [load_words(0)]
-        w4w_raw = keep.tile([P, PASSES, 2 * H // 4], U32, name="w4w_raw")
-        nc.sync.dma_start(out=w4w_raw[:].bitcast(I32), in_=w4_words.rearrange("a p c -> p a c").bitcast(I32))
         w4s_raw = keep.tile([P, PASSES, H // 4], U32, name="w4s_raw")
         for q in range(4):
             nc.sync.dma_start(
@@ -68,6 +66,8 @@ def tile_list_claim_triage_urgency_kernel(
                 in_=w4_scales[:, 4 * q : 4 * q + 4, :].rearrange("a r c -> r a c").bitcast(I32),
             )
         tab.append(load_words(1))
+        w4w_raw = keep.tile([P, PASSES, 2 * H // 4], U32, name="w4w_raw")
+        nc.sync.dma_start(out=w4w_raw[:].bitcast(I32), in_=w4_words.rearrange("a p c -> p a c").bitcast(I32))
 
         picked_sc = keep.tile([P, S // 4], I32, name="picked_sc", tag="picked_sc", align_bytes=64)
         nc.vector.tensor_copy(picked_sc[:].bitcast(U8), tab_sc[:].bitcast(U8).indirect(idx[:]))
@@ -215,7 +215,7 @@ def tile_list_claim_triage_urgency_kernel(
         out_rows = out.rearrange("(i p) j -> p i j", p=P)
 
         def second_stage(a2, half, bank_tag):
-            grouped = work.tile([P, HALF, PACK], BF16, name="a2_grouped", align_bytes=64)
+            grouped = keep.tile([P, HALF, PACK], BF16, name="a2_grouped", tag="a2_grouped%d" % half, align_bytes=64)
             nc.scalar.copy(out=grouped[:], in_=a2[:].rearrange("p t j -> p j t"))
             codes = work.tile([P, HALF], U32, name="a2_codes", align_bytes=64)
             scales = work.tile([P, HALF], U8, name="a2_scales", align_bytes=64)
@@ -239,17 +239,22 @@ def tile_list_claim_triage_urgency_kernel(
                 banks.append(acc)
             return banks
 
-        def finish(banks, half):
+        def finish(acc, half, first_tile, tiles, tag):
             span = slice(half * HALF, (half + 1) * HALF)
-            for b, acc in enumerate(banks):
-                result = work.tile([P, 2, HALF], F32, name="result", bufs=6)
-                nc.vector.tensor_tensor(result[:], acc[:], desk_sb[:, 2 * b : 2 * b + 2, span], ALU.add)
-                nc.sync.dma_start(out=out_rows[:, 2 * b : 2 * b + 2, span], in_=result[:])
+            rows = slice(first_tile, first_tile + tiles)
+            result = keep.tile([P, tiles, HALF], F32, name="result", tag=tag, align_bytes=64)
+            nc.vector.tensor_tensor(result[:], acc, desk_sb[:, rows, span], ALU.add)
+            nc.sync.dma_start(out=out_rows[:, rows, span], in_=result[:])
 
         first_banks = second_stage(a2_first, 0, "second")
         a2_second = keep.tile([P, PACK, HALF], F32, name="a2_second", tag="source")
         for t in range(PACK):
             kept_pairs(a2_second, t, 1)
         second_banks = second_stage(a2_second, 1, "first")
-        finish(first_banks, 0)
-        finish(second_banks, 1)
+        finish(first_banks[0][:], 0, 0, 2, "result0")
+        finish(first_banks[1][:], 0, 2, 2, "result1")
+        finish(first_banks[2][:], 0, 4, 2, "a2_grouped1")
+        finish(second_banks[0][:], 1, 0, 2, "result2")
+        finish(second_banks[1][:], 1, 2, 2, "result3")
+        finish(second_banks[2][:, 0:1, :], 1, 4, 1, "result4")
+        finish(second_banks[2][:, 1:2, :], 1, 5, 1, "result5")

@@ -114,19 +114,22 @@ def tile_list_claim_triage_urgency_kernel(
         w1_scales = keep.tile([P, PACK * PASSES * P], U8, name="w1_scales", align_bytes=64)
 
         def quantise_w1(t):
-            grouped = keep.tile([P, PASSES, P * PACK], BF16, name="w1_grouped", tag="tab1", align_bytes=64)
+            grouped = keep.tile([P, PASSES * P * PACK], BF16, name="w1_grouped", tag="tab1", align_bytes=64)
             interleave = nc.vector.tensor_copy if t == 0 else nc.scalar.copy
+            calls = PASSES if t == 0 else 1
+            width = PASSES * P // calls
             for a in range(PASSES):
                 interleave(
-                    out=grouped[:, a, :].rearrange("p (g u j) -> p g u j", u=8, j=PACK),
+                    out=grouped[:, a * P * PACK : (a + 1) * P * PACK].rearrange("p (g u j) -> p g u j", u=8, j=PACK),
                     in_=w1_raw[:, a].rearrange("p j (g t u) -> p t g u j", t=PACK, u=8)[:, t],
                 )
-            span = slice(t * PASSES * P, (t + 1) * PASSES * P)
-            nc.vector.quantize_mx(
-                out=w1_codes[:, span].bitcast(FP8X4),
-                scales=w1_scales[:, span],
-                in_=grouped[:].rearrange("p a c -> p (a c)"),
-            )
+            for i in range(calls):
+                span = slice(t * PASSES * P + i * width, t * PASSES * P + (i + 1) * width)
+                nc.vector.quantize_mx(
+                    out=w1_codes[:, span].bitcast(FP8X4),
+                    scales=w1_scales[:, span],
+                    in_=grouped[:, i * width * PACK : (i + 1) * width * PACK],
+                )
 
         def product(acc, weights, weight_scales, c):
             for a in range(PASSES):

from contextlib import ExitStack

import concourse.mybir as mybir

K, T, S, PAIRS, KEPT, H, N = 1024, 4096, 2048, 1024, 512, 512, 768
FLOPS = 2 * (2 * K * H * S + H * N * KEPT)

F32 = mybir.dt.float32
BF16 = mybir.dt.bfloat16
I32 = mybir.dt.int32
U32 = mybir.dt.uint32
U16 = mybir.dt.uint16
U8 = mybir.dt.uint8
FP8X4 = mybir.dt.float8_e4m3fn_x4
FP4X4 = mybir.dt.float4_e2m1fn_x4
ALU = mybir.AluOpType
ACT = mybir.ActivationFunctionType

P = 128
PACK = 4
PASSES = K // (P * PACK)
BANK = 512
CHUNKS = S // BANK
HALF = KEPT // 2
N_TILES = N // P
LIST_ROWS = 16
SCALE_ROWS = 16


def tile_list_claim_triage_urgency_kernel(
    tc, tab_words, tab_scales, offs, pos1, pos2, pos3, pos4, w1, w4_words, w4_scales, trust, w2, desk, out
):
    nc = tc.nc
    with ExitStack() as ctx:
        lists = ctx.enter_context(tc.tile_pool(name="lists", bufs=1))
        keep = ctx.enter_context(tc.tile_pool(name="keep", bufs=1))
        work = ctx.enter_context(tc.tile_pool(name="work", bufs=2))
        psum = ctx.enter_context(tc.psum_pool(name="psum", bufs=4))

        def load_list(src, name):
            tile = lists.tile([P, src.shape[1]], U16, name=name)
            nc.sync.dma_start(tile[:], src)
            return tile

        idx = load_list(offs, "idx")
        tab_sc = keep.tile([P, T // 4], I32, name="tab_sc", tag="tab_sc", align_bytes=64)
        nc.sync.dma_start(
            out=tab_sc[P - PASSES * SCALE_ROWS : P, :], in_=tab_scales.rearrange("a q t -> q a t").bitcast(I32)
        )
        nc.vector.memset(tab_sc[0 : P - PASSES * SCALE_ROWS, :], 0)
        p2 = load_list(pos2, "p2")
        p4 = load_list(pos4, "p4")
        p1 = load_list(pos1, "p1")
        p3 = load_list(pos3, "p3")

        def load_words(a):
            words = keep.tile([P, T], I32, name="tab%d" % a, tag="tab%d" % a, align_bytes=64)
            nc.sync.dma_start(out=words[:], in_=tab_words[a].rearrange("p t i -> p (t i)").bitcast(I32))
            return words

        tab = [load_words(0)]
        w4s_raw = keep.tile([P, PASSES, H // 4], U32, name="w4s_raw")
        for q in range(4):
            nc.sync.dma_start(
                out=w4s_raw[32 * q : 32 * q + 4, :, :].bitcast(I32),
                in_=w4_scales[:, 4 * q : 4 * q + 4, :].rearrange("a r c -> r a c").bitcast(I32),
            )
        tab.append(load_words(1))
        w4w_raw = keep.tile([P, PASSES, 2 * H // 4], U32, name="w4w_raw")
        nc.sync.dma_start(out=w4w_raw[:].bitcast(I32), in_=w4_words.rearrange("a p c -> p a c").bitcast(I32))

        picked_sc = keep.tile([P, S // 4], I32, name="picked_sc", tag="picked_sc", align_bytes=64)
        nc.vector.tensor_copy(picked_sc[:].bitcast(U8), tab_sc[:].bitcast(U8).indirect(idx[:]))
        planes = keep.tile([P, PASSES * S // 4], I32, name="planes", align_bytes=64)
        nc.vector.memset(planes[:], 0)
        for q in range(4):
            nc.sync.dma_start(out=planes[32 * q : 32 * q + 4, :], in_=picked_sc[96 + 8 * q : 96 + 8 * q + 8, :])
        v_scales = planes[:].bitcast(U8)
        w1_raw = keep.tile([P, PASSES, PACK, H], F32, name="w1_raw", tag="tab_sc", align_bytes=64)
        for a in range(PASSES):
            nc.sync.dma_start(
                out=w1_raw[:, a], in_=w1[a * 512 : (a + 1) * 512, :].rearrange("(p j) c -> p j c", j=PACK)
            )

        trust_sb = keep.tile([P, PACK, 8], F32, name="trust_sb", tag="picked_sc", align_bytes=64)
        for t in range(PACK):
            with nc.allow_non_contiguous_dma(reason="one float a partition"):
                nc.sync.dma_start(out=trust_sb[:, t, 0:1], in_=trust.rearrange("(g t u) -> t g u", t=PACK, u=8)[t])

        picked = [keep.tile([P, S], U32, name="picked%d" % a, align_bytes=64) for a in range(PASSES)]
        nc.vector.tensor_copy(picked[0][:], tab[0][:].bitcast(U32).indirect(idx[:]))
        cols = BANK // LIST_ROWS
        for c in range(CHUNKS):
            nc.vector.tensor_copy(
                picked[1][:, c * BANK : (c + 1) * BANK],
                tab[1][:].bitcast(U32).indirect(idx[:, c * cols : (c + 1) * cols]),
            )

        w4w = keep.tile([P, PASSES, 2 * H // 4], U32, name="w4w", align_bytes=64)
        nc.scalar.copy(
            out=w4w[:].rearrange("p a (t g w) -> p a t g w", t=PACK, w=4),
            in_=w4w_raw[:].rearrange("p a (g t w) -> p a t g w", t=PACK, w=4),
        )
        w4s = keep.tile([P, PASSES, H // 4], U32, name="w4s", align_bytes=64)
        nc.vector.memset(w4s[:], 0)
        for q in range(4):
            rows = slice(32 * q, 32 * q + 4)
            nc.scalar.copy(
                out=w4s[rows, :, :].rearrange("p a (t g w) -> p a t g w", t=PACK, w=2),
                in_=w4s_raw[rows, :, :].rearrange("p a (g t w) -> p a t g w", t=PACK, w=2),
            )

        w1_codes = keep.tile([P, PACK * PASSES * P], U32, name="w1_codes", align_bytes=64)
        w1_scales = keep.tile([P, PACK * PASSES * P], U8, name="w1_scales", align_bytes=64)

        def quantise_w1(t):
            grouped = keep.tile([P, PASSES * P * PACK], BF16, name="w1_grouped", tag="tab1", align_bytes=64)
            interleave = nc.vector.tensor_copy if t == 0 else nc.scalar.copy
            calls = PASSES if t == 0 else 1
            width = PASSES * P // calls
            for a in range(PASSES):
                interleave(
                    out=grouped[:, a * P * PACK : (a + 1) * P * PACK].rearrange("p (g u j) -> p g u j", u=8, j=PACK),
                    in_=w1_raw[:, a].rearrange("p j (g t u) -> p t g u j", t=PACK, u=8)[:, t],
                )
            for i in range(calls):
                span = slice(t * PASSES * P + i * width, t * PASSES * P + (i + 1) * width)
                nc.vector.quantize_mx(
                    out=w1_codes[:, span].bitcast(FP8X4),
                    scales=w1_scales[:, span],
                    in_=grouped[:, i * width * PACK : (i + 1) * width * PACK],
                )

        def product(acc, weights, weight_scales, c):
            for a in range(PASSES):
                nc.tensor.matmul_mx(
                    out=acc[:],
                    lhsT=weights(a),
                    lhsT_scale=weight_scales(a),
                    rhs=picked[a][:, c * BANK : (c + 1) * BANK].bitcast(FP8X4),
                    rhs_scale=v_scales[:, a * S + c * BANK : a * S + (c + 1) * BANK],
                    start=(a == 0),
                    stop=(a == PASSES - 1),
                )

        a2_first = keep.tile([P, PACK, HALF], F32, name="a2_first")
        half_cols = HALF // LIST_ROWS
        a1_tiles, earlier_tiles = [], []

        def kept_pairs(a2, t, half):
            nc.vector.tensor_tensor(
                a2[:, t, :],
                a1_tiles[t][:].indirect(p3[:, half * half_cols : (half + 1) * half_cols]),
                earlier_tiles[t][:, half * HALF : (half + 1) * HALF],
                ALU.subtract,
            )

        quantise_w1(0)
        for t in range(PACK):
            h = keep.tile([P, S], F32, name="h%d" % t)
            for c in range(CHUNKS):
                acc4 = psum.tile([P, BANK], F32, name="acc4", tag="first")
                product(
                    acc4,
                    lambda a: w4w[:, a, 64 * t : 64 * (t + 1)].bitcast(FP4X4),
                    lambda a: w4s[:, a, 32 * t : 32 * (t + 1)].bitcast(U8),
                    c,
                )
                nc.scalar.copy(out=h[:, c * BANK : (c + 1) * BANK], in_=acc4[:])
            for c in range(CHUNKS):
                span = slice(c * BANK, (c + 1) * BANK)
                acc1 = psum.tile([P, BANK], F32, name="acc1", tag="first")
                product(
                    acc1,
                    lambda a: w1_codes[:, (t * PASSES + a) * P : (t * PASSES + a + 1) * P].bitcast(FP8X4),
                    lambda a: w1_scales[:, (t * PASSES + a) * P : (t * PASSES + a + 1) * P],
                    c,
                )
                nc.vector.tensor_tensor(h[:, span], acc1[:], h[:, span], ALU.max)
            if t + 1 < PACK:
                quantise_w1(t + 1)

            if t > 0:
                kept_pairs(a2_first, t - 1, 0)

            partner = work.tile([P, PAIRS], F32, name="partner")
            nc.vector.tensor_copy(partner[:], h[:].indirect(p2[:]))
            source = keep.tile([P, PAIRS], F32, name="source", tag="source")
            nc.scalar.activation(out=source[:], in_=partner[:], func=ACT.Tanh, scale=trust_sb[:, t, 0:1])
            earlier = keep.tile([P, KEPT], F32, name="earlier%d" % t)
            nc.vector.tensor_copy(earlier[:], h[:].indirect(p4[:]))
            a1 = keep.tile([P, PAIRS], F32, name="a1_%d" % t)
            nc.vector.tensor_tensor(a1[:], h[:].indirect(p1[:]), source[:], ALU.mult)
            a1_tiles.append(a1)
            earlier_tiles.append(earlier)

        kept_pairs(a2_first, PACK - 1, 0)

        w2_raw = keep.tile([P, PACK, N], F32, name="w2_raw", tag="tab_sc", align_bytes=64)
        for t in range(PACK):
            nc.sync.dma_start(out=w2_raw[:, t, :], in_=w2.rearrange("(g t u) n -> t g u n", t=PACK, u=8)[t])
        desk_sb = keep.tile([P, N_TILES, KEPT], F32, name="desk_sb", tag="tab1", align_bytes=64)
        nc.sync.dma_start(out=desk_sb[:], in_=desk.rearrange("(i p) j -> p i j", p=P))
        w2_grouped = keep.tile([P, N, PACK], BF16, name="w2_grouped", align_bytes=64)
        for i in range(N_TILES):
            span = slice(i * P, (i + 1) * P)
            nc.scalar.copy(out=w2_grouped[:, span, :], in_=w2_raw[:, :, span].rearrange("p t n -> p n t"))
        w2_codes = keep.tile([P, N], U32, name="w2_codes", align_bytes=64)
        w2_scales = keep.tile([P, N], U8, name="w2_scales", align_bytes=64)
        for i in range(2):
            span = slice(i * N // 2, (i + 1) * N // 2)
            nc.vector.quantize_mx(
                out=w2_codes[:, span].bitcast(FP8X4),
                scales=w2_scales[:, span],
                in_=w2_grouped[:, span, :].rearrange("p n t -> p (n t)"),
            )

        out_rows = out.rearrange("(i p) j -> p i j", p=P)

        def second_stage(a2, half, bank_tag):
            grouped = keep.tile([P, HALF, PACK], BF16, name="a2_grouped", tag="a2_grouped%d" % half, align_bytes=64)
            nc.scalar.copy(out=grouped[:], in_=a2[:].rearrange("p t j -> p j t"))
            codes = work.tile([P, HALF], U32, name="a2_codes", align_bytes=64)
            scales = work.tile([P, HALF], U8, name="a2_scales", align_bytes=64)
            nc.vector.quantize_mx(
                out=codes[:].bitcast(FP8X4), scales=scales[:], in_=grouped[:].rearrange("p j t -> p (j t)")
            )
            banks = []
            for b in range(N_TILES // 2):
                acc = psum.tile([P, 2, HALF], F32, name="acc2", tag=bank_tag)
                for e in range(2):
                    span = slice((2 * b + e) * P, (2 * b + e + 1) * P)
                    nc.tensor.matmul_mx(
                        out=acc[:, e, :],
                        lhsT=w2_codes[:, span].bitcast(FP8X4),
                        lhsT_scale=w2_scales[:, span],
                        rhs=codes[:].bitcast(FP8X4),
                        rhs_scale=scales[:],
                        start=True,
                        stop=True,
                    )
                banks.append(acc)
            return banks

        def finish(acc, half, first_tile, tiles, tag):
            span = slice(half * HALF, (half + 1) * HALF)
            rows = slice(first_tile, first_tile + tiles)
            result = keep.tile([P, tiles, HALF], F32, name="result", tag=tag, align_bytes=64)
            nc.vector.tensor_tensor(result[:], acc, desk_sb[:, rows, span], ALU.add)
            nc.sync.dma_start(out=out_rows[:, rows, span], in_=result[:])

        first_banks = second_stage(a2_first, 0, "second")
        a2_second = keep.tile([P, PACK, HALF], F32, name="a2_second", tag="source")
        for t in range(PACK):
            kept_pairs(a2_second, t, 1)
        second_banks = second_stage(a2_second, 1, "first")
        finish(first_banks[0][:], 0, 0, 2, "result0")
        finish(first_banks[1][:], 0, 2, 2, "result1")
        finish(first_banks[2][:], 0, 4, 2, "a2_grouped1")
        finish(second_banks[0][:], 1, 0, 2, "result2")
        finish(second_banks[1][:], 1, 2, 2, "result3")
        finish(second_banks[2][:, 0:1, :], 1, 4, 1, "result4")
        finish(second_banks[2][:, 1:2, :], 1, 5, 1, "result5")
